import numpy as np
CORES = [2,10,18,26,34,42,50,58,66,74,82,90,98,106,114,122]
N = 16
def setup_inputs(rng):
    return {"x": rng.standard_normal((N, 128, 256), dtype=np.float32)}
def reference(x):
    s = x.sum(axis=0, dtype=np.float64).astype(x.dtype)
    s = np.maximum(s, 0)
    return {"y": np.broadcast_to(s, (N,) + s.shape)}

@@ -1,0 +1,88 @@
+import concourse.bass as bass
+
+SCRATCH = {
+    "xd": ("dram", [16, 128, 16], "float32"),
+    "land": ("dram", [16, 128, 16], "float32"),
+    "sumd": ("dram", [128, 16], "float32"),
+    "zerod": ("dram", [128, 16], "float32"),
+    "zs": ("sbuf", [128, 16], "float32"),
+    "yd": ("dram", [16, 128, 16], "float32"),
+}
+SEMAPHORES = ["ld1", "ld2", "sent", "arr", "sarr", "ms", "zd", "ysame", "yoth", "st1", "st2"]
+
+RANK_K = 2
+ADD_K = 1
+
+
+def send_k(chip):
+    return 3 if chip % 2 == 0 else 7
+
+
+def slice_of(chip):
+    return (chip % 2) * 8 + chip // 2
+
+
+def rank_program(g, core, T, topo):
+    S = T.sem
+    chip = topo.chip(core)
+    k = core % 8
+    par = chip % 2
+    chips = [topo.chip(c) for c in T.cores]
+    same = [c for c in chips if c % 2 == par and c != chip]
+    other = [c for c in chips if c % 2 != par and not topo.mates(c, chip)] + [chip ^ 1]
+
+    def did(c):
+        a = topo.addr(c)
+        return bass.DstId(rid=a[0], pnc=a[1])
+
+    if k == RANK_K:
+        rank = T.rank_of(core)
+        sh, oh = 8 * par, 8 * (1 - par)
+        g.sync.dma_start(T.xd[oh:oh + 8], T.x[8 * oh:8 * oh + 64, :]).then_inc(S.ld1, 16)
+        g.sync.dma_start(T.xd[sh:sh + 8], T.x[8 * sh:8 * sh + 64, :]).then_inc(S.ld2, 16)
+        g.wait_ge(S.ld1, 16)
+        g.remote_dma_fused([
+            bass.RemoteDMATransfer(dst_ids=[did(c * 8 + ADD_K)], dma_engine_mask=1 << j, remote_sem=S.arr,
+                                   src=T.xd[slice_of(c)], dst=T.land[rank])
+            for j, c in enumerate(other)], local_sem=S.sent)
+        g.wait_ge(S.ld2, 16)
+        g.remote_dma_fused([
+            bass.RemoteDMATransfer(dst_ids=[did(c * 8 + ADD_K)], dma_engine_mask=1 << j, remote_sem=S.arr,
+                                   src=T.xd[slice_of(c)], dst=T.land[rank])
+            for j, c in enumerate(same)] + [
+            bass.RemoteDMATransfer(dst_ids=[did(chip * 8 + ADD_K)], dma_engine_mask=0xFF00, remote_sem=S.arr,
+                                   src=T.xd[slice_of(chip)], dst=T.land[rank])], local_sem=S.sent)
+        g.wait_ge(S.ysame, 7 * 4 + 8)
+        g.dma_start(T.y[8 * sh:8 * sh + 64, :], T.yd[sh:sh + 8]).then_inc(S.st1, 16)
+        g.sync.wait_ge(S.yoth, 8 * 4)
+        g.sync.dma_start(T.y[8 * oh:8 * oh + 64, :], T.yd[oh:oh + 8]).then_inc(S.st2, 16)
+        g.wait_ge(S.sent, 8 + 7 + 8)
+        g.wait_ge(S.st1, 16)
+        g.wait_ge(S.st2, 16)
+        return
+
+    if k == ADD_K:
+        g.wait_ge(S.arr, 15 + 8)
+        g.remote_dma_fused([
+            bass.RemoteDMATransfer(dst_ids=[did(chip * 8 + send_k(chip))], dma_engine_mask=0xFFFF, remote_sem=S.sarr,
+                                   srcs=[T.land[i] for i in range(16)], dsts=[T.sumd[:]], alu_op=1)],
+            local_sem=S.sent)
+        g.wait_ge(S.sent, 16)
+        return
+
+    if k == send_k(chip):
+        s = slice_of(chip)
+        g.vector.memset(T.zs[:], 0.0).then_inc(S.ms, 1)
+        g.sync.wait_ge(S.ms, 1)
+        g.sync.dma_start(T.zerod[:], T.zs[:]).then_inc(S.zd, 16)
+        g.wait_ge(S.zd, 16)
+        g.wait_ge(S.sarr, 16)
+
+        def tr(dst_chips, mask, sem):
+            return bass.RemoteDMATransfer(dst_ids=[did(c * 8 + RANK_K) for c in dst_chips], dma_engine_mask=mask,
+                                          remote_sem=sem, srcs=[T.sumd[:], T.zerod[:]],
+                                          dsts=[T.yd[s] for c in dst_chips], alu_op=2)
+        g.remote_dma_fused([tr(other, 0x0F, S.yoth), tr(same, 0xF0, S.ysame), tr([chip], 0xFF00, S.ysame)],
+                           local_sem=S.sent)
+        g.wait_ge(S.sent, 4 + 4 + 8)
+        return

@@ -5,21 +5,34 @@ SCRATCH = {
     "land": ("dram", [16, 128, 16], "float32"),
     "sumd": ("dram", [128, 16], "float32"),
     "zerod": ("dram", [128, 16], "float32"),
-    "zs": ("sbuf", [128, 16], "float32"),
+    "zs": ("sbuf", [128, 256], "float32"),
     "yd": ("dram", [16, 128, 16], "float32"),
 }
 SEMAPHORES = ["ld1", "ld2", "sent", "arr", "sarr", "ms", "zd", "ysame", "yoth", "st1", "st2"]
 
 RANK_K = 2
 ADD_K = 1
-
-
-def send_k(chip):
-    return 3 if chip % 2 == 0 else 7
+SEND_KS = (3, 7)
 
 
 def slice_of(chip):
     return (chip % 2) * 8 + chip // 2
+
+
+def deal(chip, k):
+    par, i = chip % 2, chip // 2
+
+    def sm(d):
+        return 2 * ((i + d) % 8) + par
+
+    def ot(d):
+        return 2 * ((i + d) % 8) + 1 - par
+
+    hv = ([sm(d) for d in (1, 2, 3, 4)], [ot(d) for d in (1, 2, 3, 4)], False)
+    lt = ([sm(d) for d in (5, 6, 7)], [ot(d) for d in (5, 6, 7, 0)], True)
+    if par == 0:
+        return {3: hv, 7: lt}[k]
+    return {7: hv, 3: lt}[k]
 
 
 def rank_program(g, core, T, topo):
@@ -35,6 +48,7 @@ def rank_program(g, core, T, topo):
         a = topo.addr(c)
         return bass.DstId(rid=a[0], pnc=a[1])
 
+    sent = 0
     if k == RANK_K:
         rank = T.rank_of(core)
         sh, oh = 8 * par, 8 * (1 - par)
@@ -52,29 +66,24 @@ def rank_program(g, core, T, topo):
             for j, c in enumerate(same)] + [
             bass.RemoteDMATransfer(dst_ids=[did(chip * 8 + ADD_K)], dma_engine_mask=0xFF00, remote_sem=S.arr,
                                    src=T.xd[slice_of(chip)], dst=T.land[rank])], local_sem=S.sent)
-        g.wait_ge(S.ysame, 7 * 4 + 8)
-        g.dma_start(T.y[8 * sh:8 * sh + 64, :], T.yd[sh:sh + 8]).then_inc(S.st1, 16)
-        g.sync.wait_ge(S.yoth, 8 * 4)
-        g.sync.dma_start(T.y[8 * oh:8 * oh + 64, :], T.yd[oh:oh + 8]).then_inc(S.st2, 16)
-        g.wait_ge(S.sent, 8 + 7 + 8)
-        g.wait_ge(S.st1, 16)
-        g.wait_ge(S.st2, 16)
-        return
+        sent += 8 + 7 + 8
 
     if k == ADD_K:
         g.wait_ge(S.arr, 15 + 8)
         g.remote_dma_fused([
-            bass.RemoteDMATransfer(dst_ids=[did(chip * 8 + send_k(chip))], dma_engine_mask=0xFFFF, remote_sem=S.sarr,
-                                   srcs=[T.land[i] for i in range(16)], dsts=[T.sumd[:]], alu_op=1)],
+            bass.RemoteDMATransfer(dst_ids=[did(chip * 8 + q) for q in SEND_KS], dma_engine_mask=0xFFFF,
+                                   remote_sem=S.sarr, srcs=[T.land[i] for i in range(16)],
+                                   dsts=[T.sumd[:] for q in SEND_KS], alu_op=1)],
             local_sem=S.sent)
         g.wait_ge(S.sent, 16)
         return
 
-    if k == send_k(chip):
+    if k in SEND_KS:
         s = slice_of(chip)
-        g.vector.memset(T.zs[:], 0.0).then_inc(S.ms, 1)
+        to_same, to_other, to_self = deal(chip, k)
+        g.vector.memset(T.zs[0:8, :], 0.0).then_inc(S.ms, 1)
         g.sync.wait_ge(S.ms, 1)
-        g.sync.dma_start(T.zerod[:], T.zs[:]).then_inc(S.zd, 16)
+        g.sync.dma_start(T.zerod[:], T.zs[0:8, :]).then_inc(S.zd, 16)
         g.wait_ge(S.zd, 16)
         g.wait_ge(S.sarr, 16)
 
@@ -82,7 +91,19 @@ def rank_program(g, core, T, topo):
             return bass.RemoteDMATransfer(dst_ids=[did(c * 8 + RANK_K) for c in dst_chips], dma_engine_mask=mask,
                                           remote_sem=sem, srcs=[T.sumd[:], T.zerod[:]],
                                           dsts=[T.yd[s] for c in dst_chips], alu_op=2)
-        g.remote_dma_fused([tr(other, 0x0F, S.yoth), tr(same, 0xF0, S.ysame), tr([chip], 0xFF00, S.ysame)],
-                           local_sem=S.sent)
-        g.wait_ge(S.sent, 4 + 4 + 8)
-        return
+        trs = [tr(to_other, 0x0F, S.yoth), tr(to_same, 0xF0, S.ysame)]
+        sent += 8
+        if to_self:
+            trs.append(tr([chip], 0xFF00, S.ysame))
+            sent += 8
+        g.remote_dma_fused(trs, local_sem=S.sent)
+
+    if k == RANK_K:
+        g.wait_ge(S.ysame, 7 * 4 + 8)
+        g.dma_start(T.y[8 * sh:8 * sh + 64, :], T.yd[sh:sh + 8]).then_inc(S.st1, 16)
+        g.sync.wait_ge(S.yoth, 8 * 4)
+        g.sync.dma_start(T.y[8 * oh:8 * oh + 64, :], T.yd[oh:oh + 8]).then_inc(S.st2, 16)
+        g.wait_ge(S.st1, 16)
+        g.wait_ge(S.st2, 16)
+    if sent:
+        g.wait_ge(S.sent, sent)

@@ -99,8 +99,8 @@ def rank_program(g, core, T, topo):
         g.remote_dma_fused(trs, local_sem=S.sent)
 
     if k == RANK_K:
-        g.wait_ge(S.ysame, 7 * 4 + 8)
-        g.dma_start(T.y[8 * sh:8 * sh + 64, :], T.yd[sh:sh + 8]).then_inc(S.st1, 16)
+        g.sync.wait_ge(S.ysame, 7 * 4 + 8)
+        g.sync.dma_start(T.y[8 * sh:8 * sh + 64, :], T.yd[sh:sh + 8]).then_inc(S.st1, 16)
         g.sync.wait_ge(S.yoth, 8 * 4)
         g.sync.dma_start(T.y[8 * oh:8 * oh + 64, :], T.yd[oh:oh + 8]).then_inc(S.st2, 16)
         g.wait_ge(S.st1, 16)

@@ -12,7 +12,10 @@ SEMAPHORES = ["ld1", "ld2", "sent", "arr", "sarr", "ms", "zd", "ysame", "yoth", 
 
 RANK_K = 2
 ADD_K = 1
-SEND_KS = (3, 7)
+
+
+def senders(chip):
+    return (3, 7) if chip % 2 == 0 else (7, 3)
 
 
 def slice_of(chip):
@@ -28,11 +31,9 @@ def deal(chip, k):
     def ot(d):
         return 2 * ((i + d) % 8) + 1 - par
 
-    hv = ([sm(d) for d in (1, 2, 3, 4)], [ot(d) for d in (1, 2, 3, 4)], False)
-    lt = ([sm(d) for d in (5, 6, 7)], [ot(d) for d in (5, 6, 7, 0)], True)
-    if par == 0:
-        return {3: hv, 7: lt}[k]
-    return {7: hv, 3: lt}[k]
+    if k == senders(chip)[0]:
+        return [sm(d) for d in (1, 2, 3, 4)], [ot(d) for d in (1, 2, 3, 4)], False
+    return [sm(d) for d in (5, 6, 7)], [ot(d) for d in (5, 6, 7, 0)], True
 
 
 def rank_program(g, core, T, topo):
@@ -48,7 +49,6 @@ def rank_program(g, core, T, topo):
         a = topo.addr(c)
         return bass.DstId(rid=a[0], pnc=a[1])
 
-    sent = 0
     if k == RANK_K:
         rank = T.rank_of(core)
         sh, oh = 8 * par, 8 * (1 - par)
@@ -66,19 +66,26 @@ def rank_program(g, core, T, topo):
             for j, c in enumerate(same)] + [
             bass.RemoteDMATransfer(dst_ids=[did(chip * 8 + ADD_K)], dma_engine_mask=0xFF00, remote_sem=S.arr,
                                    src=T.xd[slice_of(chip)], dst=T.land[rank])], local_sem=S.sent)
-        sent += 8 + 7 + 8
+        g.sync.wait_ge(S.ysame, 7 * 4 + 8)
+        g.sync.dma_start(T.y[8 * sh:8 * sh + 64, :], T.yd[sh:sh + 8]).then_inc(S.st1, 16)
+        g.sync.wait_ge(S.yoth, 8 * 4)
+        g.sync.dma_start(T.y[8 * oh:8 * oh + 64, :], T.yd[oh:oh + 8]).then_inc(S.st2, 16)
+        g.wait_ge(S.sent, 8 + 7 + 8)
+        g.wait_ge(S.st1, 16)
+        g.wait_ge(S.st2, 16)
+        return
 
     if k == ADD_K:
         g.wait_ge(S.arr, 15 + 8)
         g.remote_dma_fused([
-            bass.RemoteDMATransfer(dst_ids=[did(chip * 8 + q) for q in SEND_KS], dma_engine_mask=0xFFFF,
+            bass.RemoteDMATransfer(dst_ids=[did(chip * 8 + q) for q in senders(chip)], dma_engine_mask=0xFFFF,
                                    remote_sem=S.sarr, srcs=[T.land[i] for i in range(16)],
-                                   dsts=[T.sumd[:] for q in SEND_KS], alu_op=1)],
+                                   dsts=[T.sumd[:] for q in senders(chip)], alu_op=1)],
             local_sem=S.sent)
         g.wait_ge(S.sent, 16)
         return
 
-    if k in SEND_KS:
+    if k in senders(chip):
         s = slice_of(chip)
         to_same, to_other, to_self = deal(chip, k)
         g.vector.memset(T.zs[0:8, :], 0.0).then_inc(S.ms, 1)
@@ -92,18 +99,7 @@ def rank_program(g, core, T, topo):
                                           remote_sem=sem, srcs=[T.sumd[:], T.zerod[:]],
                                           dsts=[T.yd[s] for c in dst_chips], alu_op=2)
         trs = [tr(to_other, 0x0F, S.yoth), tr(to_same, 0xF0, S.ysame)]
-        sent += 8
         if to_self:
             trs.append(tr([chip], 0xFF00, S.ysame))
-            sent += 8
         g.remote_dma_fused(trs, local_sem=S.sent)
-
-    if k == RANK_K:
-        g.sync.wait_ge(S.ysame, 7 * 4 + 8)
-        g.sync.dma_start(T.y[8 * sh:8 * sh + 64, :], T.yd[sh:sh + 8]).then_inc(S.st1, 16)
-        g.sync.wait_ge(S.yoth, 8 * 4)
-        g.sync.dma_start(T.y[8 * oh:8 * oh + 64, :], T.yd[oh:oh + 8]).then_inc(S.st2, 16)
-        g.wait_ge(S.st1, 16)
-        g.wait_ge(S.st2, 16)
-    if sent:
-        g.wait_ge(S.sent, sent)
+        g.wait_ge(S.sent, 16 if to_self else 8)

import concourse.bass as bass

SCRATCH = {
    "xd": ("dram", [16, 128, 16], "float32"),
    "land": ("dram", [16, 128, 16], "float32"),
    "sumd": ("dram", [128, 16], "float32"),
    "zerod": ("dram", [128, 16], "float32"),
    "zs": ("sbuf", [128, 256], "float32"),
    "yd": ("dram", [16, 128, 16], "float32"),
}
SEMAPHORES = ["ld1", "ld2", "sent", "arr", "sarr", "ms", "zd", "ysame", "yoth", "st1", "st2"]

RANK_K = 2
ADD_K = 1


def senders(chip):
    return (3, 7) if chip % 2 == 0 else (7, 3)


def slice_of(chip):
    return (chip % 2) * 8 + chip // 2


def deal(chip, k):
    par, i = chip % 2, chip // 2

    def sm(d):
        return 2 * ((i + d) % 8) + par

    def ot(d):
        return 2 * ((i + d) % 8) + 1 - par

    if k == senders(chip)[0]:
        return [sm(d) for d in (1, 2, 3, 4)], [ot(d) for d in (1, 2, 3, 4)], False
    return [sm(d) for d in (5, 6, 7)], [ot(d) for d in (5, 6, 7, 0)], True


def rank_program(g, core, T, topo):
    S = T.sem
    chip = topo.chip(core)
    k = core % 8
    par = chip % 2
    chips = [topo.chip(c) for c in T.cores]
    same = [c for c in chips if c % 2 == par and c != chip]
    other = [c for c in chips if c % 2 != par and not topo.mates(c, chip)] + [chip ^ 1]

    def did(c):
        a = topo.addr(c)
        return bass.DstId(rid=a[0], pnc=a[1])

    if k == RANK_K:
        rank = T.rank_of(core)
        sh, oh = 8 * par, 8 * (1 - par)
        g.sync.dma_start(T.xd[oh:oh + 8], T.x[8 * oh:8 * oh + 64, :]).then_inc(S.ld1, 16)
        g.sync.dma_start(T.xd[sh:sh + 8], T.x[8 * sh:8 * sh + 64, :]).then_inc(S.ld2, 16)
        g.wait_ge(S.ld1, 16)
        g.remote_dma_fused([
            bass.RemoteDMATransfer(dst_ids=[did(c * 8 + ADD_K)], dma_engine_mask=1 << j, remote_sem=S.arr,
                                   src=T.xd[slice_of(c)], dst=T.land[rank])
            for j, c in enumerate(other)], local_sem=S.sent)
        g.wait_ge(S.ld2, 16)
        g.remote_dma_fused([
            bass.RemoteDMATransfer(dst_ids=[did(c * 8 + ADD_K)], dma_engine_mask=1 << j, remote_sem=S.arr,
                                   src=T.xd[slice_of(c)], dst=T.land[rank])
            for j, c in enumerate(same)] + [
            bass.RemoteDMATransfer(dst_ids=[did(chip * 8 + ADD_K)], dma_engine_mask=0xFF00, remote_sem=S.arr,
                                   src=T.xd[slice_of(chip)], dst=T.land[rank])], local_sem=S.sent)
        g.sync.wait_ge(S.ysame, 7 * 4 + 8)
        g.sync.dma_start(T.y[8 * sh:8 * sh + 64, :], T.yd[sh:sh + 8]).then_inc(S.st1, 16)
        g.sync.wait_ge(S.yoth, 8 * 4)
        g.sync.dma_start(T.y[8 * oh:8 * oh + 64, :], T.yd[oh:oh + 8]).then_inc(S.st2, 16)
        g.wait_ge(S.sent, 8 + 7 + 8)
        g.wait_ge(S.st1, 16)
        g.wait_ge(S.st2, 16)
        return

    if k == ADD_K:
        g.wait_ge(S.arr, 15 + 8)
        g.remote_dma_fused([
            bass.RemoteDMATransfer(dst_ids=[did(chip * 8 + q) for q in senders(chip)], dma_engine_mask=0xFFFF,
                                   remote_sem=S.sarr, srcs=[T.land[i] for i in range(16)],
                                   dsts=[T.sumd[:] for q in senders(chip)], alu_op=1)],
            local_sem=S.sent)
        g.wait_ge(S.sent, 16)
        return

    if k in senders(chip):
        s = slice_of(chip)
        to_same, to_other, to_self = deal(chip, k)
        g.vector.memset(T.zs[0:8, :], 0.0).then_inc(S.ms, 1)
        g.sync.wait_ge(S.ms, 1)
        g.sync.dma_start(T.zerod[:], T.zs[0:8, :]).then_inc(S.zd, 16)
        g.wait_ge(S.zd, 16)
        g.wait_ge(S.sarr, 16)

        def tr(dst_chips, mask, sem):
            return bass.RemoteDMATransfer(dst_ids=[did(c * 8 + RANK_K) for c in dst_chips], dma_engine_mask=mask,
                                          remote_sem=sem, srcs=[T.sumd[:], T.zerod[:]],
                                          dsts=[T.yd[s] for c in dst_chips], alu_op=2)
        trs = [tr(to_other, 0x0F, S.yoth), tr(to_same, 0xF0, S.ysame)]
        if to_self:
            trs.append(tr([chip], 0xFF00, S.ysame))
        g.remote_dma_fused(trs, local_sem=S.sent)
        g.wait_ge(S.sent, 16 if to_self else 8)
